import numpy as np
import ml_dtypes


def mxq(x, axis, fmt="e4m3"):
    dtype, down = {"e4m3": (ml_dtypes.float8_e4m3fn, 7), "e5m2": (ml_dtypes.float8_e5m2, 14)}[fmt]
    v = np.moveaxis(np.asarray(x, np.float32).astype(ml_dtypes.bfloat16).astype(np.float64), axis, -1)
    blocks = v.reshape(v.shape[:-1] + (-1, 32))
    amax = np.abs(blocks).max(-1, keepdims=True)
    byte = np.maximum(np.where(amax > 0, np.frexp(amax)[1] - 1 + 127, 0) - down, 1)
    scale = np.exp2(byte - 127.0)
    codes = (blocks / scale).astype(np.float32).astype(dtype).astype(np.float64)
    return np.moveaxis((codes * scale).reshape(v.shape), -1, axis)


WIDE = False


def mx_kscale(k):
    if not WIDE:
        return np.ones(k)
    levels = np.array([30, -30])
    if k % 512:
        return np.exp2(np.random.permutation(np.resize(levels, k // 32))).repeat(32)
    a = np.empty((k // 512, 16))
    for p in range(k // 512):
        a[p, :8] = np.random.permutation(np.resize(levels, 8))
        for g in range(8):
            far = levels[np.abs(levels - a[p, g]) >= 10]
            a[p, g + 8] = far[np.random.randint(len(far))]
    return np.exp2(a.ravel()).repeat(32)


def f64(x):
    return np.asarray(x).astype(np.float64)


def striped(idx):
    return np.tile(np.asarray(idx).reshape(-1, 16).T, (8, 1)).astype(np.uint16)


def unstriped(offs):
    return offs[:16].T.reshape(-1).astype(np.int64)


E2M1 = np.array([0.0, 0.5, 1.0, 1.5, 2.0, 3.0, 4.0, 6.0, -0.0, -0.5, -1.0, -1.5, -2.0, -3.0, -4.0, -6.0])


def pack_weight(w, fmt):
    k, n = w.shape
    w = f64(np.asarray(w, np.float32).astype(ml_dtypes.bfloat16)).reshape(k // 32, 32, n)
    amax = np.abs(w).max(1)
    if fmt in ("e4m3", "e5m2"):
        byte = np.frexp(amax)[1] - 1 + 127 - (7 if fmt == "e4m3" else 14)
    else:
        mant, ex = np.frexp(amax / 6.0)
        byte = np.where(mant > 0.5, ex, ex - 1) + 127
    byte = np.clip(np.where(amax > 0, byte, 1), 1, 254)
    scaled = (w * np.exp2(127.0 - byte)[:, None, :]).reshape(k, n).astype(np.float32)
    by_word = np.ascontiguousarray(scaled.reshape(k // 512, 128, 4, n).transpose(0, 1, 3, 2))
    if fmt in ("e4m3", "e5m2"):
        words = by_word.astype(ml_dtypes.float8_e4m3fn if fmt == "e4m3" else ml_dtypes.float8_e5m2).view(np.uint8)
    else:
        c = by_word.astype(ml_dtypes.float4_e2m1fn).view(np.uint8) & 0xF
        words = (c[..., 0::2] | (c[..., 1::2] << 4)).reshape(k // 512, 128, 2 * n)
    return np.ascontiguousarray(words), np.ascontiguousarray(byte.astype(np.uint8).reshape(k // 512, 16, n))


def unpack_weight(words, scales, fmt):
    g, _, n = scales.shape
    words = np.ascontiguousarray(words).reshape(g, 128, n, -1)
    if fmt in ("e4m3", "e5m2"):
        vals = words.view(ml_dtypes.float8_e4m3fn if fmt == "e4m3" else ml_dtypes.float8_e5m2).astype(np.float64)
    else:
        nib = np.empty((g, 128, n, 4), np.uint8)
        nib[..., 0::2] = words & 0xF
        nib[..., 1::2] = words >> 4
        vals = E2M1[nib]
    vals = vals * np.repeat(np.exp2(scales.astype(np.float64) - 127.0), 8, axis=1)[..., None]
    return vals.transpose(0, 1, 3, 2).reshape(g * 512, n)


K, T, J, R, L, N = 512, 1024, 256, 512, 512, 256


def setup_inputs():
    n = np.random.standard_normal
    idx = np.random.permutation(T)[:J]
    fk = mx_kscale(K)
    fr = mx_kscale(R)
    fl = mx_kscale(L)
    xtp = pack_weight(n((K, T)) / fk[:, None], "e5m2")
    wp = pack_weight(n((K, R)) * 1 / np.sqrt(K) * fk[:, None] * fr, "e4m3")
    sxp = pack_weight(n((L, J)) / fl[:, None], "e2m1")
    wsp = pack_weight(n((L, R)) * 1 / np.sqrt(L) * fl[:, None] * fr, "e2m1")
    wbp = pack_weight(n((R, N)) * 1 / np.sqrt(R) / fr[:, None], "e2m1")
    return {
        "xt_words": xtp[0],
        "xt_scales": xtp[1],
        "w_words": wp[0],
        "w_scales": wp[1],
        "sx_words": sxp[0],
        "sx_scales": sxp[1],
        "ws_words": wsp[0],
        "ws_scales": wsp[1],
        "wb_words": wbp[0],
        "wb_scales": wbp[1],
        "rs": (1.0 * n((J, N))).astype(np.float32),
        "offs": striped(idx),
    }


def reference(xt_words, xt_scales, w_words, w_scales, sx_words, sx_scales, ws_words, ws_scales, wb_words, wb_scales, rs, offs):
    idx = unstriped(offs)
    xtu = unpack_weight(xt_words, xt_scales, "e5m2")
    wu = unpack_weight(w_words, w_scales, "e4m3")
    sxu = unpack_weight(sx_words, sx_scales, "e2m1")
    wsu = unpack_weight(ws_words, ws_scales, "e2m1")
    wbu = unpack_weight(wb_words, wb_scales, "e2m1")
    xtidxg = xtu[:, idx]
    a = wu.T @ xtidxg
    b2 = wsu.T @ sxu
    hid = np.maximum(a, b2)
    hidq = mxq(hid, 0, "e5m2")
    p = hidq.T @ wbu
    pk2 = np.max(np.abs(p), axis=1, keepdims=True)
    y = p / (pk2 + 0.2) + 0.3 * f64(rs)
    return y

@@ -1,0 +1,164 @@
+from contextlib import ExitStack
+
+import concourse.mybir as mybir
+
+K, T, J, R, L, N = 512, 1024, 256, 512, 512, 256
+FLOPS = 2 * (K * R * J + L * R * J + R * J * N)
+
+F32 = mybir.dt.float32
+BF16 = mybir.dt.bfloat16
+I32 = mybir.dt.int32
+U32 = mybir.dt.uint32
+U16 = mybir.dt.uint16
+U8 = mybir.dt.uint8
+E4M3 = mybir.dt.float8_e4m3fn_x4
+E5M2 = mybir.dt.float8_e5m2_x4
+E2M1 = mybir.dt.float4_e2m1fn_x4
+ALU = mybir.AluOpType
+ACT = mybir.ActivationFunctionType
+
+P = 128
+PACK = 4
+HALF = 128
+HALVES = J // HALF
+
+
+def load_scale_rows(queue, plane, scales, quadrants=range(4)):
+    for q in quadrants:
+        queue.dma_start(out=plane[32 * q : 32 * q + 4, :].bitcast(I32), in_=scales[0, 4 * q : 4 * q + 4, :].bitcast(I32))
+
+
+def deal_columns(nc, dst, src, run):
+    nc.vector.tensor_copy(
+        out=dst.rearrange("p (t c i) -> p c t i", t=PACK, i=run),
+        in_=src.rearrange("p (c i t) -> p c t i", t=PACK, i=run),
+    )
+
+
+def tile_list_picked_rival_rowpeaks_kernel(
+    tc, xt_words, xt_scales, w_words, w_scales, sx_words, sx_scales, ws_words, ws_scales, wb_words, wb_scales, rs, offs, out
+):
+    nc = tc.nc
+    with ExitStack() as ctx:
+        keep = ctx.enter_context(tc.tile_pool(name="keep", bufs=1))
+        psum = ctx.enter_context(tc.psum_pool(name="psum", bufs=1))
+
+        offsets = keep.tile([P, J // 16], U16, name="offsets")
+        xt_w = keep.tile([P, T], I32, name="xt_w", align_bytes=64)
+        xt_s = keep.tile([P, T], U8, name="xt_s", align_bytes=64)
+        w_raw = keep.tile([P, R], I32, name="w_raw", tag="first", align_bytes=64)
+        ws_raw = keep.tile([P, 2 * R], U8, name="ws_raw", tag="second", align_bytes=64)
+        sx_w = keep.tile([P, 2 * J], U8, name="sx_w", align_bytes=64)
+        ws_s_raw = keep.tile([P, R], U8, name="ws_s_raw", align_bytes=64)
+        planes = keep.tile([P, R + J + N], U8, name="planes", align_bytes=64)
+        w_s_raw = planes[:, 0:R]
+        sx_s = planes[:, R : R + J]
+        wb_s = planes[:, R + J : R + J + N]
+
+        nc.vector.memset(ws_s_raw[:].bitcast(I32), 0)
+        nc.vector.memset(planes[:].bitcast(I32), 0)
+        nc.vector.memset(xt_s[:].bitcast(I32), 0)
+
+        nc.gpsimd.dma_start(out=xt_w[:], in_=xt_words[0].rearrange("p n t -> p (n t)").bitcast(I32))
+        load_scale_rows(nc.gpsimd, xt_s, xt_scales, [3])
+        nc.sync.dma_start(out=ws_raw[:].bitcast(I32), in_=ws_words[0].bitcast(I32))
+        nc.sync.dma_start(out=sx_w[:].bitcast(I32), in_=sx_words[0].bitcast(I32))
+        nc.sync.dma_start(offsets[:], offs)
+        load_scale_rows(nc.sync, ws_s_raw, ws_scales)
+        nc.sync.dma_start(out=w_raw[:], in_=w_words[0].rearrange("p n t -> p (n t)").bitcast(I32))
+        load_scale_rows(nc.sync, sx_s, sx_scales)
+        load_scale_rows(nc.sync, xt_s, xt_scales, [0, 1, 2])
+        load_scale_rows(nc.sync, w_s_raw, w_scales)
+        load_scale_rows(nc.sync, wb_s, wb_scales)
+
+        ws_w = keep.tile([P, 2 * R], U8, name="ws_w", align_bytes=64)
+        ws_s = keep.tile([P, R], U8, name="ws_s", align_bytes=64)
+        w_w = keep.tile([P, R], I32, name="w_w", align_bytes=64)
+        w_s = keep.tile([P, R], U8, name="w_s", align_bytes=64)
+        deal_columns(nc, ws_w[:].bitcast(U16), ws_raw[:].bitcast(U16), 8)
+        deal_columns(nc, ws_s[:], ws_s_raw[:], 16)
+        deal_columns(nc, w_w[:].bitcast(U32), w_raw[:].bitcast(U32), 4)
+
+        wb_w = keep.tile([P, 2 * N], U8, name="wb_w", tag="second", align_bytes=64)
+        rs_sb = keep.tile([P, HALVES, N], F32, name="rs_sb", tag="first", align_bytes=64)
+        nc.sync.dma_start(out=wb_w[:].bitcast(I32), in_=wb_words[0].bitcast(I32))
+        nc.sync.dma_start(out=rs_sb[:], in_=rs.rearrange("(h p) n -> p h n", p=P))
+
+        xg_s = keep.tile([P, J], U8, name="xg_s", align_bytes=64)
+        nc.vector.tensor_copy(out=xg_s[:], in_=xt_s[:].indirect(offsets[:]))
+        xg_w = []
+        for h in range(HALVES):
+            g = keep.tile([P, HALF], U32, name="xg_w%d" % h, align_bytes=64)
+            cols = HALF // 16
+            nc.vector.tensor_copy(out=g[:], in_=xt_w[:].bitcast(U32).indirect(offsets[:, h * cols : (h + 1) * cols]))
+            xg_w.append(g)
+        deal_columns(nc, w_s[:], w_s_raw, 16)
+
+        b_sb = []
+        a_ps = []
+        for h in range(HALVES):
+            b = psum.tile([P, PACK, HALF], F32, name="b_ps%d" % h)
+            for t in range(PACK):
+                nc.tensor.matmul_mx(
+                    out=b[:, t, :],
+                    lhsT=ws_w[:, 2 * t * P : 2 * (t + 1) * P].bitcast(E2M1),
+                    lhsT_scale=ws_s[:, t * P : (t + 1) * P],
+                    rhs=sx_w[:, 2 * h * HALF : 2 * (h + 1) * HALF].bitcast(E2M1),
+                    rhs_scale=sx_s[:, h * HALF : (h + 1) * HALF],
+                    start=True,
+                    stop=True,
+                )
+            kept = keep.tile([P, HALF, PACK], F32, name="b_sb%d" % h, align_bytes=64)
+            nc.scalar.activation(out=kept[:], in_=b[:].rearrange("p t j -> p j t"), func=ACT.Copy)
+            b_sb.append(kept)
+        for h in range(HALVES):
+            a = psum.tile([P, PACK, HALF], F32, name="a_ps%d" % h)
+            for t in range(PACK):
+                nc.tensor.matmul_mx(
+                    out=a[:, t, :],
+                    lhsT=w_w[:, t * P : (t + 1) * P].bitcast(E4M3),
+                    lhsT_scale=w_s[:, t * P : (t + 1) * P],
+                    rhs=xg_w[h][:].bitcast(E5M2),
+                    rhs_scale=xg_s[:, h * HALF : (h + 1) * HALF],
+                    start=True,
+                    stop=True,
+                )
+            a_ps.append(a)
+
+        rs_scaled = keep.tile([P, HALVES, N], F32, name="rs_scaled", align_bytes=64)
+        nc.scalar.activation(out=rs_scaled[:], in_=rs_sb[:], func=ACT.Copy, scale=0.3)
+
+        p_ps = []
+        for h in range(HALVES):
+            hid = keep.tile([P, HALF, PACK], BF16, name="hid%d" % h, align_bytes=64)
+            nc.vector.tensor_tensor(out=hid[:], in0=a_ps[h][:].rearrange("p t j -> p j t"), in1=b_sb[h][:], op=ALU.max)
+            hid_w = keep.tile([P, HALF], U32, name="hid_w%d" % h, align_bytes=64)
+            hid_s = keep.tile([P, HALF], U8, name="hid_s%d" % h, align_bytes=64)
+            nc.vector.quantize_mx(out=hid_w[:].bitcast(E5M2), scales=hid_s[:], in_=hid[:].rearrange("p j t -> p (j t)"))
+            p = psum.tile([P, N], F32, name="p_ps%d" % h)
+            nc.tensor.matmul_mx(
+                out=p[:],
+                lhsT=hid_w[:].bitcast(E5M2),
+                lhsT_scale=hid_s[:],
+                rhs=wb_w[:].bitcast(E2M1),
+                rhs_scale=wb_s,
+                start=True,
+                stop=True,
+            )
+            p_ps.append(p)
+
+        for h in range(HALVES):
+            mag = keep.tile([P, N], F32, name="mag%d" % h)
+            nc.scalar.activation(out=mag[:], in_=p_ps[h][:], func=ACT.Abs)
+            shifted = keep.tile([P, N], F32, name="shifted%d" % h)
+            denom = keep.tile([P, 1], F32, name="denom%d" % h)
+            nc.vector.tensor_scalar(
+                out=shifted[:], in0=mag[:], scalar1=0.2, scalar2=None, op0=ALU.add, op1=ALU.max, accum_out=denom[:]
+            )
+            inv = keep.tile([P, 1], F32, name="inv%d" % h)
+            nc.vector.reciprocal(out=inv[:], in_=denom[:])
+            y = keep.tile([P, N], F32, name="y%d" % h)
+            nc.vector.scalar_tensor_tensor(
+                out=y[:], in0=p_ps[h][:], scalar=inv[:], in1=rs_scaled[:, h, :], op0=ALU.mult, op1=ALU.add
+            )
+            nc.sync.dma_start(out=out[h * HALF : (h + 1) * HALF, :], in_=y[:])

@@ -23,15 +23,15 @@ HALF = 128
 HALVES = J // HALF
 
 
-def load_scale_rows(queue, plane, scales, quadrants=range(4)):
-    for q in quadrants:
-        queue.dma_start(out=plane[32 * q : 32 * q + 4, :].bitcast(I32), in_=scales[0, 4 * q : 4 * q + 4, :].bitcast(I32))
+def load_scale_rows(queue, plane, scales, rows=range(4)):
+    for r in rows:
+        queue.dma_start(out=plane[r:P:32, :].bitcast(I32), in_=scales[0, r:16:4, :].bitcast(I32))
 
 
-def deal_columns(nc, dst, src, run):
+def deal_columns(nc, dst, src, run, slots=slice(0, PACK)):
     nc.vector.tensor_copy(
-        out=dst.rearrange("p (t c i) -> p c t i", t=PACK, i=run),
-        in_=src.rearrange("p (c i t) -> p c t i", t=PACK, i=run),
+        out=dst.rearrange("p (t c i) -> p c t i", t=PACK, i=run)[:, :, slots, :],
+        in_=src.rearrange("p (c i t) -> p c t i", t=PACK, i=run)[:, :, slots, :],
     )
 
 
@@ -49,7 +49,7 @@ def tile_list_picked_rival_rowpeaks_kernel(
         w_raw = keep.tile([P, R], I32, name="w_raw", tag="first", align_bytes=64)
         ws_raw = keep.tile([P, 2 * R], U8, name="ws_raw", tag="second", align_bytes=64)
         sx_w = keep.tile([P, 2 * J], U8, name="sx_w", align_bytes=64)
-        ws_s_raw = keep.tile([P, R], U8, name="ws_s_raw", align_bytes=64)
+        ws_s_raw = keep.tile([P, R], U8, name="ws_s_raw", tag="third", align_bytes=64)
         planes = keep.tile([P, R + J + N], U8, name="planes", align_bytes=64)
         w_s_raw = planes[:, 0:R]
         sx_s = planes[:, R : R + J]
@@ -60,15 +60,15 @@ def tile_list_picked_rival_rowpeaks_kernel(
         nc.vector.memset(xt_s[:].bitcast(I32), 0)
 
         nc.gpsimd.dma_start(out=xt_w[:], in_=xt_words[0].rearrange("p n t -> p (n t)").bitcast(I32))
-        load_scale_rows(nc.gpsimd, xt_s, xt_scales, [3])
-        nc.sync.dma_start(out=ws_raw[:].bitcast(I32), in_=ws_words[0].bitcast(I32))
+        load_scale_rows(nc.gpsimd, w_s_raw, w_scales, [3])
         nc.sync.dma_start(out=sx_w[:].bitcast(I32), in_=sx_words[0].bitcast(I32))
+        nc.sync.dma_start(out=ws_raw[:].bitcast(I32), in_=ws_words[0].bitcast(I32))
         nc.sync.dma_start(offsets[:], offs)
         load_scale_rows(nc.sync, ws_s_raw, ws_scales)
         nc.sync.dma_start(out=w_raw[:], in_=w_words[0].rearrange("p n t -> p (n t)").bitcast(I32))
         load_scale_rows(nc.sync, sx_s, sx_scales)
-        load_scale_rows(nc.sync, xt_s, xt_scales, [0, 1, 2])
-        load_scale_rows(nc.sync, w_s_raw, w_scales)
+        load_scale_rows(nc.sync, xt_s, xt_scales)
+        load_scale_rows(nc.sync, w_s_raw, w_scales, [0, 1, 2])
         load_scale_rows(nc.sync, wb_s, wb_scales)
 
         ws_w = keep.tile([P, 2 * R], U8, name="ws_w", align_bytes=64)
@@ -84,15 +84,15 @@ def tile_list_picked_rival_rowpeaks_kernel(
         nc.sync.dma_start(out=wb_w[:].bitcast(I32), in_=wb_words[0].bitcast(I32))
         nc.sync.dma_start(out=rs_sb[:], in_=rs.rearrange("(h p) n -> p h n", p=P))
 
+        xg_all = keep.tile([P, J], U32, name="xg_all", tag="third", align_bytes=64)
+        xg_w = [xg_all[:, h * HALF : (h + 1) * HALF] for h in range(HALVES)]
+        for h in range(HALVES):
+            cols = HALF // 16
+            nc.vector.tensor_copy(out=xg_w[h], in_=xt_w[:].bitcast(U32).indirect(offsets[:, h * cols : (h + 1) * cols]))
         xg_s = keep.tile([P, J], U8, name="xg_s", align_bytes=64)
         nc.vector.tensor_copy(out=xg_s[:], in_=xt_s[:].indirect(offsets[:]))
-        xg_w = []
-        for h in range(HALVES):
-            g = keep.tile([P, HALF], U32, name="xg_w%d" % h, align_bytes=64)
-            cols = HALF // 16
-            nc.vector.tensor_copy(out=g[:], in_=xt_w[:].bitcast(U32).indirect(offsets[:, h * cols : (h + 1) * cols]))
-            xg_w.append(g)
-        deal_columns(nc, w_s[:], w_s_raw, 16)
+        deal_columns(nc, w_s[:], w_s_raw, 16, slice(0, 2))
+        deal_columns(nc, w_s[:], w_s_raw, 16, slice(2, 4))
 
         b_sb = []
         a_ps = []
@@ -118,7 +118,7 @@ def tile_list_picked_rival_rowpeaks_kernel(
                     out=a[:, t, :],
                     lhsT=w_w[:, t * P : (t + 1) * P].bitcast(E4M3),
                     lhsT_scale=w_s[:, t * P : (t + 1) * P],
-                    rhs=xg_w[h][:].bitcast(E5M2),
+                    rhs=xg_w[h].bitcast(E5M2),
                     rhs_scale=xg_s[:, h * HALF : (h + 1) * HALF],
                     start=True,
                     stop=True,
@@ -128,10 +128,14 @@ def tile_list_picked_rival_rowpeaks_kernel(
         rs_scaled = keep.tile([P, HALVES, N], F32, name="rs_scaled", align_bytes=64)
         nc.scalar.activation(out=rs_scaled[:], in_=rs_sb[:], func=ACT.Copy, scale=0.3)
 
-        p_ps = []
+        hids = []
         for h in range(HALVES):
             hid = keep.tile([P, HALF, PACK], BF16, name="hid%d" % h, align_bytes=64)
             nc.vector.tensor_tensor(out=hid[:], in0=a_ps[h][:].rearrange("p t j -> p j t"), in1=b_sb[h][:], op=ALU.max)
+            hids.append(hid)
+        p_ps = []
+        for h in range(HALVES):
+            hid = hids[h]
             hid_w = keep.tile([P, HALF], U32, name="hid_w%d" % h, align_bytes=64)
             hid_s = keep.tile([P, HALF], U8, name="hid_s%d" % h, align_bytes=64)
             nc.vector.quantize_mx(out=hid_w[:].bitcast(E5M2), scales=hid_s[:], in_=hid[:].rearrange("p j t -> p (j t)"))

@@ -43,59 +43,76 @@ def tile_list_picked_rival_rowpeaks_kernel(
         keep = ctx.enter_context(tc.tile_pool(name="keep", bufs=1))
         psum = ctx.enter_context(tc.psum_pool(name="psum", bufs=1))
 
+        shared = ctx.enter_context(tc.tile_pool(name="shared", bufs=1))
         offsets = keep.tile([P, J // 16], U16, name="offsets")
-        xt_w = keep.tile([P, T], I32, name="xt_w", align_bytes=64)
-        xt_s = keep.tile([P, T], U8, name="xt_s", align_bytes=64)
-        w_raw = keep.tile([P, R], I32, name="w_raw", tag="first", align_bytes=64)
+        xt_w = keep.tile([P, T], I32, name="xt_w", tag="fourth", align_bytes=64)
+        xt_s = keep.tile([P, T], U8, name="xt_s", tag="third", align_bytes=64)
+        w_raw = shared.tile([P, R], I32, name="w_raw", offset=0, align_bytes=64)
         ws_raw = keep.tile([P, 2 * R], U8, name="ws_raw", tag="second", align_bytes=64)
         sx_w = keep.tile([P, 2 * J], U8, name="sx_w", align_bytes=64)
-        ws_s_raw = keep.tile([P, R], U8, name="ws_s_raw", tag="third", align_bytes=64)
+        w_s_raw = keep.tile([P, R], U8, name="w_s_raw", tag="fifth", align_bytes=64)
         planes = keep.tile([P, R + J + N], U8, name="planes", align_bytes=64)
-        w_s_raw = planes[:, 0:R]
+        ws_s_raw = planes[:, 0:R]
         sx_s = planes[:, R : R + J]
         wb_s = planes[:, R + J : R + J + N]
 
-        nc.vector.memset(ws_s_raw[:].bitcast(I32), 0)
-        nc.vector.memset(planes[:].bitcast(I32), 0)
         nc.vector.memset(xt_s[:].bitcast(I32), 0)
+        nc.vector.memset(w_s_raw[:].bitcast(I32), 0)
+        nc.vector.memset(planes[:].bitcast(I32), 0)
 
         nc.gpsimd.dma_start(out=xt_w[:], in_=xt_words[0].rearrange("p n t -> p (n t)").bitcast(I32))
-        load_scale_rows(nc.gpsimd, w_s_raw, w_scales, [3])
+        load_scale_rows(nc.gpsimd, sx_s, sx_scales, [3, 2])
         nc.sync.dma_start(out=sx_w[:].bitcast(I32), in_=sx_words[0].bitcast(I32))
         nc.sync.dma_start(out=ws_raw[:].bitcast(I32), in_=ws_words[0].bitcast(I32))
         nc.sync.dma_start(offsets[:], offs)
-        load_scale_rows(nc.sync, ws_s_raw, ws_scales)
-        nc.sync.dma_start(out=w_raw[:], in_=w_words[0].rearrange("p n t -> p (n t)").bitcast(I32))
-        load_scale_rows(nc.sync, sx_s, sx_scales)
         load_scale_rows(nc.sync, xt_s, xt_scales)
-        load_scale_rows(nc.sync, w_s_raw, w_scales, [0, 1, 2])
+        nc.sync.dma_start(out=w_raw[:], in_=w_words[0].rearrange("p n t -> p (n t)").bitcast(I32))
+        load_scale_rows(nc.sync, w_s_raw, w_scales)
+        load_scale_rows(nc.sync, ws_s_raw, ws_scales)
+        load_scale_rows(nc.sync, sx_s, sx_scales, [0, 1])
         load_scale_rows(nc.sync, wb_s, wb_scales)
 
         ws_w = keep.tile([P, 2 * R], U8, name="ws_w", align_bytes=64)
-        ws_s = keep.tile([P, R], U8, name="ws_s", align_bytes=64)
         w_w = keep.tile([P, R], I32, name="w_w", align_bytes=64)
-        w_s = keep.tile([P, R], U8, name="w_s", align_bytes=64)
+        xg_s = keep.tile([P, J], U8, name="xg_s", align_bytes=64)
         deal_columns(nc, ws_w[:].bitcast(U16), ws_raw[:].bitcast(U16), 8)
-        deal_columns(nc, ws_s[:], ws_s_raw[:], 16)
+        nc.vector.tensor_copy(out=xg_s[:], in_=xt_s[:].indirect(offsets[:]))
         deal_columns(nc, w_w[:].bitcast(U32), w_raw[:].bitcast(U32), 4)
 
         wb_w = keep.tile([P, 2 * N], U8, name="wb_w", tag="second", align_bytes=64)
-        rs_sb = keep.tile([P, HALVES, N], F32, name="rs_sb", tag="first", align_bytes=64)
+        rs_sb = keep.tile([P, HALVES, N], F32, name="rs_sb", tag="third", align_bytes=64)
         nc.sync.dma_start(out=wb_w[:].bitcast(I32), in_=wb_words[0].bitcast(I32))
         nc.sync.dma_start(out=rs_sb[:], in_=rs.rearrange("(h p) n -> p h n", p=P))
 
-        xg_all = keep.tile([P, J], U32, name="xg_all", tag="third", align_bytes=64)
-        xg_w = [xg_all[:, h * HALF : (h + 1) * HALF] for h in range(HALVES)]
-        for h in range(HALVES):
-            cols = HALF // 16
-            nc.vector.tensor_copy(out=xg_w[h], in_=xt_w[:].bitcast(U32).indirect(offsets[:, h * cols : (h + 1) * cols]))
-        xg_s = keep.tile([P, J], U8, name="xg_s", align_bytes=64)
-        nc.vector.tensor_copy(out=xg_s[:], in_=xt_s[:].indirect(offsets[:]))
-        deal_columns(nc, w_s[:], w_s_raw, 16, slice(0, 2))
-        deal_columns(nc, w_s[:], w_s_raw, 16, slice(2, 4))
+        picks = [offsets[:, h * HALF // 16 : (h + 1) * HALF // 16] for h in range(HALVES)]
+        xg_w0 = shared.tile([P, HALF], U32, name="xg_w0", offset=0, align_bytes=64)
+        w_s = shared.tile([P, R], U8, name="w_s", offset=4 * HALF, align_bytes=64)
+        nc.vector.tensor_copy(out=xg_w0[:], in_=xt_w[:].bitcast(U32).indirect(picks[0]))
+        deal_columns(nc, w_s[:], w_s_raw[:], 16, slice(0, 2))
+        deal_columns(nc, w_s[:], w_s_raw[:], 16, slice(2, 4))
+        xg_w1 = keep.tile([P, HALF], U32, name="xg_w1", tag="fifth", align_bytes=64)
+        nc.vector.tensor_copy(out=xg_w1[:], in_=xt_w[:].bitcast(U32).indirect(picks[1]))
+        xg_w = [xg_w0[:], xg_w1[:]]
+        ws_s = keep.tile([P, R], U8, name="ws_s", tag="fourth", align_bytes=64)
+        deal_columns(nc, ws_s[:], ws_s_raw, 16)
 
-        b_sb = []
-        a_ps = []
+        a_sb = []
+        b_ps = []
+        for h in range(HALVES):
+            a_ps = psum.tile([P, PACK, HALF], F32, name="a_ps%d" % h)
+            for t in range(PACK):
+                nc.tensor.matmul_mx(
+                    out=a_ps[:, t, :],
+                    lhsT=w_w[:, t * P : (t + 1) * P].bitcast(E4M3),
+                    lhsT_scale=w_s[:, t * P : (t + 1) * P],
+                    rhs=xg_w[h].bitcast(E5M2),
+                    rhs_scale=xg_s[:, h * HALF : (h + 1) * HALF],
+                    start=True,
+                    stop=True,
+                )
+            a = keep.tile([P, HALF, PACK], F32, name="a_sb%d" % h, align_bytes=64)
+            nc.scalar.activation(out=a[:], in_=a_ps[:].rearrange("p t j -> p j t"), func=ACT.Copy)
+            a_sb.append(a)
         for h in range(HALVES):
             b = psum.tile([P, PACK, HALF], F32, name="b_ps%d" % h)
             for t in range(PACK):
@@ -108,22 +125,7 @@ def tile_list_picked_rival_rowpeaks_kernel(
                     start=True,
                     stop=True,
                 )
-            kept = keep.tile([P, HALF, PACK], F32, name="b_sb%d" % h, align_bytes=64)
-            nc.scalar.activation(out=kept[:], in_=b[:].rearrange("p t j -> p j t"), func=ACT.Copy)
-            b_sb.append(kept)
-        for h in range(HALVES):
-            a = psum.tile([P, PACK, HALF], F32, name="a_ps%d" % h)
-            for t in range(PACK):
-                nc.tensor.matmul_mx(
-                    out=a[:, t, :],
-                    lhsT=w_w[:, t * P : (t + 1) * P].bitcast(E4M3),
-                    lhsT_scale=w_s[:, t * P : (t + 1) * P],
-                    rhs=xg_w[h].bitcast(E5M2),
-                    rhs_scale=xg_s[:, h * HALF : (h + 1) * HALF],
-                    start=True,
-                    stop=True,
-                )
-            a_ps.append(a)
+            b_ps.append(b)
 
         rs_scaled = keep.tile([P, HALVES, N], F32, name="rs_scaled", align_bytes=64)
         nc.scalar.activation(out=rs_scaled[:], in_=rs_sb[:], func=ACT.Copy, scale=0.3)
@@ -131,7 +133,7 @@ def tile_list_picked_rival_rowpeaks_kernel(
         hids = []
         for h in range(HALVES):
             hid = keep.tile([P, HALF, PACK], BF16, name="hid%d" % h, align_bytes=64)
-            nc.vector.tensor_tensor(out=hid[:], in0=a_ps[h][:].rearrange("p t j -> p j t"), in1=b_sb[h][:], op=ALU.max)
+            nc.vector.tensor_tensor(out=hid[:], in0=b_ps[h][:].rearrange("p t j -> p j t"), in1=a_sb[h][:], op=ALU.max)
             hids.append(hid)
         p_ps = []
         for h in range(HALVES):

from contextlib import ExitStack

import concourse.mybir as mybir

K, T, J, R, L, N = 512, 1024, 256, 512, 512, 256
FLOPS = 2 * (K * R * J + L * R * J + R * J * N)

F32 = mybir.dt.float32
BF16 = mybir.dt.bfloat16
I32 = mybir.dt.int32
U32 = mybir.dt.uint32
U16 = mybir.dt.uint16
U8 = mybir.dt.uint8
E4M3 = mybir.dt.float8_e4m3fn_x4
E5M2 = mybir.dt.float8_e5m2_x4
E2M1 = mybir.dt.float4_e2m1fn_x4
ALU = mybir.AluOpType
ACT = mybir.ActivationFunctionType

P = 128
PACK = 4
HALF = 128
HALVES = J // HALF


def load_scale_rows(queue, plane, scales, rows=range(4)):
    for r in rows:
        queue.dma_start(out=plane[r:P:32, :].bitcast(I32), in_=scales[0, r:16:4, :].bitcast(I32))


def deal_columns(nc, dst, src, run, slots=slice(0, PACK)):
    nc.vector.tensor_copy(
        out=dst.rearrange("p (t c i) -> p c t i", t=PACK, i=run)[:, :, slots, :],
        in_=src.rearrange("p (c i t) -> p c t i", t=PACK, i=run)[:, :, slots, :],
    )


def tile_list_picked_rival_rowpeaks_kernel(
    tc, xt_words, xt_scales, w_words, w_scales, sx_words, sx_scales, ws_words, ws_scales, wb_words, wb_scales, rs, offs, out
):
    nc = tc.nc
    with ExitStack() as ctx:
        keep = ctx.enter_context(tc.tile_pool(name="keep", bufs=1))
        psum = ctx.enter_context(tc.psum_pool(name="psum", bufs=1))

        shared = ctx.enter_context(tc.tile_pool(name="shared", bufs=1))
        offsets = keep.tile([P, J // 16], U16, name="offsets")
        xt_w = keep.tile([P, T], I32, name="xt_w", tag="fourth", align_bytes=64)
        xt_s = keep.tile([P, T], U8, name="xt_s", tag="third", align_bytes=64)
        w_raw = shared.tile([P, R], I32, name="w_raw", offset=0, align_bytes=64)
        ws_raw = keep.tile([P, 2 * R], U8, name="ws_raw", tag="second", align_bytes=64)
        sx_w = keep.tile([P, 2 * J], U8, name="sx_w", align_bytes=64)
        w_s_raw = keep.tile([P, R], U8, name="w_s_raw", tag="fifth", align_bytes=64)
        planes = keep.tile([P, R + J + N], U8, name="planes", align_bytes=64)
        ws_s_raw = planes[:, 0:R]
        sx_s = planes[:, R : R + J]
        wb_s = planes[:, R + J : R + J + N]

        nc.vector.memset(xt_s[:].bitcast(I32), 0)
        nc.vector.memset(w_s_raw[:].bitcast(I32), 0)
        nc.vector.memset(planes[:].bitcast(I32), 0)

        nc.gpsimd.dma_start(out=xt_w[:], in_=xt_words[0].rearrange("p n t -> p (n t)").bitcast(I32))
        load_scale_rows(nc.gpsimd, sx_s, sx_scales, [3, 2])
        nc.sync.dma_start(out=sx_w[:].bitcast(I32), in_=sx_words[0].bitcast(I32))
        nc.sync.dma_start(out=ws_raw[:].bitcast(I32), in_=ws_words[0].bitcast(I32))
        nc.sync.dma_start(offsets[:], offs)
        load_scale_rows(nc.sync, xt_s, xt_scales)
        nc.sync.dma_start(out=w_raw[:], in_=w_words[0].rearrange("p n t -> p (n t)").bitcast(I32))
        load_scale_rows(nc.sync, w_s_raw, w_scales)
        load_scale_rows(nc.sync, ws_s_raw, ws_scales)
        load_scale_rows(nc.sync, sx_s, sx_scales, [0, 1])
        load_scale_rows(nc.sync, wb_s, wb_scales)

        ws_w = keep.tile([P, 2 * R], U8, name="ws_w", align_bytes=64)
        w_w = keep.tile([P, R], I32, name="w_w", align_bytes=64)
        xg_s = keep.tile([P, J], U8, name="xg_s", align_bytes=64)
        deal_columns(nc, ws_w[:].bitcast(U16), ws_raw[:].bitcast(U16), 8)
        nc.vector.tensor_copy(out=xg_s[:], in_=xt_s[:].indirect(offsets[:]))
        deal_columns(nc, w_w[:].bitcast(U32), w_raw[:].bitcast(U32), 4)

        wb_w = keep.tile([P, 2 * N], U8, name="wb_w", tag="second", align_bytes=64)
        rs_sb = keep.tile([P, HALVES, N], F32, name="rs_sb", tag="third", align_bytes=64)
        nc.sync.dma_start(out=wb_w[:].bitcast(I32), in_=wb_words[0].bitcast(I32))
        nc.sync.dma_start(out=rs_sb[:], in_=rs.rearrange("(h p) n -> p h n", p=P))

        picks = [offsets[:, h * HALF // 16 : (h + 1) * HALF // 16] for h in range(HALVES)]
        xg_w0 = shared.tile([P, HALF], U32, name="xg_w0", offset=0, align_bytes=64)
        w_s = shared.tile([P, R], U8, name="w_s", offset=4 * HALF, align_bytes=64)
        nc.vector.tensor_copy(out=xg_w0[:], in_=xt_w[:].bitcast(U32).indirect(picks[0]))
        deal_columns(nc, w_s[:], w_s_raw[:], 16, slice(0, 2))
        deal_columns(nc, w_s[:], w_s_raw[:], 16, slice(2, 4))
        xg_w1 = keep.tile([P, HALF], U32, name="xg_w1", tag="fifth", align_bytes=64)
        nc.vector.tensor_copy(out=xg_w1[:], in_=xt_w[:].bitcast(U32).indirect(picks[1]))
        xg_w = [xg_w0[:], xg_w1[:]]
        ws_s = keep.tile([P, R], U8, name="ws_s", tag="fourth", align_bytes=64)
        deal_columns(nc, ws_s[:], ws_s_raw, 16)

        a_sb = []
        b_ps = []
        for h in range(HALVES):
            a_ps = psum.tile([P, PACK, HALF], F32, name="a_ps%d" % h)
            for t in range(PACK):
                nc.tensor.matmul_mx(
                    out=a_ps[:, t, :],
                    lhsT=w_w[:, t * P : (t + 1) * P].bitcast(E4M3),
                    lhsT_scale=w_s[:, t * P : (t + 1) * P],
                    rhs=xg_w[h].bitcast(E5M2),
                    rhs_scale=xg_s[:, h * HALF : (h + 1) * HALF],
                    start=True,
                    stop=True,
                )
            a = keep.tile([P, HALF, PACK], F32, name="a_sb%d" % h, align_bytes=64)
            nc.scalar.activation(out=a[:], in_=a_ps[:].rearrange("p t j -> p j t"), func=ACT.Copy)
            a_sb.append(a)
        for h in range(HALVES):
            b = psum.tile([P, PACK, HALF], F32, name="b_ps%d" % h)
            for t in range(PACK):
                nc.tensor.matmul_mx(
                    out=b[:, t, :],
                    lhsT=ws_w[:, 2 * t * P : 2 * (t + 1) * P].bitcast(E2M1),
                    lhsT_scale=ws_s[:, t * P : (t + 1) * P],
                    rhs=sx_w[:, 2 * h * HALF : 2 * (h + 1) * HALF].bitcast(E2M1),
                    rhs_scale=sx_s[:, h * HALF : (h + 1) * HALF],
                    start=True,
                    stop=True,
                )
            b_ps.append(b)

        rs_scaled = keep.tile([P, HALVES, N], F32, name="rs_scaled", align_bytes=64)
        nc.scalar.activation(out=rs_scaled[:], in_=rs_sb[:], func=ACT.Copy, scale=0.3)

        hids = []
        for h in range(HALVES):
            hid = keep.tile([P, HALF, PACK], BF16, name="hid%d" % h, align_bytes=64)
            nc.vector.tensor_tensor(out=hid[:], in0=b_ps[h][:].rearrange("p t j -> p j t"), in1=a_sb[h][:], op=ALU.max)
            hids.append(hid)
        p_ps = []
        for h in range(HALVES):
            hid = hids[h]
            hid_w = keep.tile([P, HALF], U32, name="hid_w%d" % h, align_bytes=64)
            hid_s = keep.tile([P, HALF], U8, name="hid_s%d" % h, align_bytes=64)
            nc.vector.quantize_mx(out=hid_w[:].bitcast(E5M2), scales=hid_s[:], in_=hid[:].rearrange("p j t -> p (j t)"))
            p = psum.tile([P, N], F32, name="p_ps%d" % h)
            nc.tensor.matmul_mx(
                out=p[:],
                lhsT=hid_w[:].bitcast(E5M2),
                lhsT_scale=hid_s[:],
                rhs=wb_w[:].bitcast(E2M1),
                rhs_scale=wb_s,
                start=True,
                stop=True,
            )
            p_ps.append(p)

        for h in range(HALVES):
            mag = keep.tile([P, N], F32, name="mag%d" % h)
            nc.scalar.activation(out=mag[:], in_=p_ps[h][:], func=ACT.Abs)
            shifted = keep.tile([P, N], F32, name="shifted%d" % h)
            denom = keep.tile([P, 1], F32, name="denom%d" % h)
            nc.vector.tensor_scalar(
                out=shifted[:], in0=mag[:], scalar1=0.2, scalar2=None, op0=ALU.add, op1=ALU.max, accum_out=denom[:]
            )
            inv = keep.tile([P, 1], F32, name="inv%d" % h)
            nc.vector.reciprocal(out=inv[:], in_=denom[:])
            y = keep.tile([P, N], F32, name="y%d" % h)
            nc.vector.scalar_tensor_tensor(
                out=y[:], in0=p_ps[h][:], scalar=inv[:], in1=rs_scaled[:, h, :], op0=ALU.mult, op1=ALU.add
            )
            nc.sync.dma_start(out=out[h * HALF : (h + 1) * HALF, :], in_=y[:])
